import numpy as np
import ml_dtypes


def mxq(x, axis, fmt="e4m3"):
    dtype, down = {"e4m3": (ml_dtypes.float8_e4m3fn, 7), "e5m2": (ml_dtypes.float8_e5m2, 14)}[fmt]
    v = np.moveaxis(np.asarray(x, np.float32).astype(ml_dtypes.bfloat16).astype(np.float64), axis, -1)
    blocks = v.reshape(v.shape[:-1] + (-1, 32))
    amax = np.abs(blocks).max(-1, keepdims=True)
    byte = np.maximum(np.where(amax > 0, np.frexp(amax)[1] - 1 + 127, 0) - down, 1)
    scale = np.exp2(byte - 127.0)
    codes = (blocks / scale).astype(np.float32).astype(dtype).astype(np.float64)
    return np.moveaxis((codes * scale).reshape(v.shape), -1, axis)


WIDE = False


def mx_kscale(k):
    if not WIDE:
        return np.ones(k)
    levels = np.array([10, -10, 5, -5, 0])
    if k % 512:
        return np.exp2(np.random.permutation(np.resize(levels, k // 32))).repeat(32)
    a = np.empty((k // 512, 16))
    for p in range(k // 512):
        a[p, :8] = np.random.permutation(np.resize(levels, 8))
        for g in range(8):
            far = levels[np.abs(levels - a[p, g]) >= 10]
            a[p, g + 8] = far[np.random.randint(len(far))]
    return np.exp2(a.ravel()).repeat(32)


def f64(x):
    return np.asarray(x).astype(np.float64)


def striped(idx):
    return np.tile(idx.reshape(-1, 16).T, (8, 1)).astype(np.uint16)


def unstriped(offs):
    return offs[:16].T.reshape(-1).astype(np.int64)


E2M1 = np.array([0.0, 0.5, 1.0, 1.5, 2.0, 3.0, 4.0, 6.0, -0.0, -0.5, -1.0, -1.5, -2.0, -3.0, -4.0, -6.0])


def pack_weight(w, fmt):
    k, n = w.shape
    w = f64(np.asarray(w, np.float32).astype(ml_dtypes.bfloat16)).reshape(k // 32, 32, n)
    amax = np.abs(w).max(1)
    if fmt == "e4m3":
        byte = np.frexp(amax)[1] - 1 + 127 - 7
    else:
        mant, ex = np.frexp(amax / 6.0)
        byte = np.where(mant > 0.5, ex, ex - 1) + 127
    byte = np.clip(np.where(amax > 0, byte, 1), 1, 254)
    scaled = (w * np.exp2(127.0 - byte)[:, None, :]).reshape(k, n).astype(np.float32)
    by_word = np.ascontiguousarray(scaled.reshape(k // 512, 128, 4, n).transpose(0, 1, 3, 2))
    if fmt == "e4m3":
        words = by_word.astype(ml_dtypes.float8_e4m3fn).view(np.uint8)
    else:
        c = by_word.astype(ml_dtypes.float4_e2m1fn).view(np.uint8) & 0xF
        words = (c[..., 0::2] | (c[..., 1::2] << 4)).reshape(k // 512, 128, 2 * n)
    return np.ascontiguousarray(words), np.ascontiguousarray(byte.astype(np.uint8).reshape(k // 512, 16, n))


def unpack_weight(words, scales, fmt):
    g, _, n = scales.shape
    words = np.ascontiguousarray(words).reshape(g, 128, n, -1)
    if fmt == "e4m3":
        vals = words.view(ml_dtypes.float8_e4m3fn).astype(np.float64)
    else:
        nib = np.empty((g, 128, n, 4), np.uint8)
        nib[..., 0::2] = words & 0xF
        nib[..., 1::2] = words >> 4
        vals = E2M1[nib]
    vals = vals * np.repeat(np.exp2(scales.astype(np.float64) - 127.0), 8, axis=1)[..., None]
    return vals.transpose(0, 1, 3, 2).reshape(g * 512, n)


def gelu(v):
    return 0.5 * v * (1.0 + np.tanh(np.sqrt(2.0 / np.pi) * (v + 0.044715 * v**3)))


K, K2, T, S, P, H, N = 1024, 512, 2048, 1024, 512, 1024, 512


def setup_inputs():
    n = np.random.standard_normal
    s = mx_kscale(K)[:, None]
    s2 = mx_kscale(K2)[:, None]
    u = mx_kscale(H)[:, None]
    tab_words, tab_scales = pack_weight(n((K, T)) * s, "e4m3")
    tab2_words, tab2_scales = pack_weight(n((K2, T)) * s2, "e4m3")
    w2_words, w2_scales = pack_weight(1.2 * n((K2, H)) / np.sqrt(K2) / s2 * u.T, "e2m1")
    w4_words, w4_scales = pack_weight(1.6 * n((H, N)) / np.sqrt(H) / u, "e4m3")
    perm = np.random.permutation(T)
    return {
        "tab_words": tab_words, "tab_scales": tab_scales,
        "tab2_words": tab2_words, "tab2_scales": tab2_scales,
        "offs": striped(np.random.permutation(T)[:S]),
        "offs2": striped(np.random.permutation(T)[:P]),
        "pos1": striped(np.random.permutation(S)[:P]),
        "offs3": striped(perm[:S]),
        "offs4": striped(perm[S:S + P]),
        "w1": (0.55 * n((K, H)) / np.sqrt(K) / s).astype(np.float32),
        "w2_words": w2_words, "w2_scales": w2_scales,
        "gain": (np.exp(0.4 * n(H)) * u[:, 0]).astype(np.float32),
        "w3": (1.6 * n((H, N)) / np.sqrt(H) / u).astype(np.float32),
        "w4_words": w4_words, "w4_scales": w4_scales,
        "resid": (0.7 * n((N, P))).astype(np.float32),
        "page1": n((N, T)).astype(np.float32),
        "wg1": np.exp(0.3 * n((128, S))).astype(np.float32),
        "wg2": np.exp(0.3 * n((128, P))).astype(np.float32)}


def reference(tab_words, tab_scales, tab2_words, tab2_scales, offs, offs2, pos1, offs3, offs4, w1, w2_words, w2_scales,
              gain, w3, w4_words, w4_scales, resid, page1, wg1, wg2):
    v = unpack_weight(tab_words, tab_scales, "e4m3")[:, unstriped(offs)]
    v2 = unpack_weight(tab2_words, tab2_scales, "e4m3")[:, unstriped(offs2)]
    h1 = np.sin(mxq(f64(w1), 0, "e4m3").T @ v)
    h2 = unpack_weight(w2_words, w2_scales, "e2m1").T @ v2
    z1 = h1 * f64(gain)[:, None]
    z2 = h2 * h1[:, unstriped(pos1)]
    y1 = mxq(f64(w3), 0, "e4m3").T @ mxq(z1, 0, "e4m3")
    y2 = (unpack_weight(w4_words, w4_scales, "e4m3").T @ mxq(z2, 0, "e4m3")) + f64(resid)
    out = f64(page1).copy()
    out[:, unstriped(offs3)] = np.tile(f64(wg1), (N // 128, 1)) * y1
    out[:, unstriped(offs4)] = np.tile(f64(wg2), (N // 128, 1)) * y2
    return out

@@ -1,0 +1,273 @@
+import math
+from contextlib import ExitStack
+
+import concourse.mybir as mybir
+
+K, K2, T, S, PK, H, N = 1024, 512, 2048, 1024, 512, 1024, 512
+FLOPS = 2 * (K * H * S + K2 * H * PK + H * N * S + H * N * PK)
+
+F32 = mybir.dt.float32
+BF16 = mybir.dt.bfloat16
+I32 = mybir.dt.int32
+U32 = mybir.dt.uint32
+U16 = mybir.dt.uint16
+U8 = mybir.dt.uint8
+FP8X4 = mybir.dt.float8_e4m3fn_x4
+FP4X4 = mybir.dt.float4_e2m1fn_x4
+ALU = mybir.AluOpType
+ACT = mybir.ActivationFunctionType
+
+P = 128
+W = 512
+
+
+def tile_list_excursion_risk_slots_kernel(
+    tc, tab_words, tab_scales, tab2_words, tab2_scales, offs, offs2, pos1, offs3, offs4,
+    w1, w2_words, w2_scales, gain, w3, w4_words, w4_scales, resid, page1, wg1, wg2, out,
+):
+    nc = tc.nc
+    with ExitStack() as ctx:
+        keep = ctx.enter_context(tc.tile_pool(name="keep", bufs=1))
+        ring = ctx.enter_context(tc.tile_pool(name="ring", bufs=2))
+        psum = ctx.enter_context(tc.psum_pool(name="psum", bufs=1))
+
+        def held(shape, dtype, name):
+            return keep.tile(shape, dtype, name=name, align_bytes=64)
+
+        def turn(shape, dtype, tag, bufs, name):
+            return ring.tile(shape, dtype, tag=tag, bufs=bufs, name=name, align_bytes=64)
+
+        def load_list(src, name):
+            tile = keep.tile(list(src.shape), U16, name=name)
+            nc.sync.dma_start(tile[:], src)
+            return tile
+
+        def load_scales(src, name, engine):
+            passes, rows, width = src.shape
+            plane = held([P, width], U8, name)
+            engine.memset(plane[:].bitcast(I32), 0)
+            return plane
+
+        def fill_scales(plane, src, queue):
+            passes = src.shape[0]
+            for q in range(4):
+                queue.dma_start(
+                    out=plane[32 * q : 32 * q + 4 * passes, :].bitcast(I32),
+                    in_=src[:, 4 * q : 4 * q + 4, :].bitcast(I32),
+                )
+
+        def load_words(src, a, name):
+            tile = turn([P, T], I32, "wide", 8, name)
+            nc.sync.dma_start(out=tile[:], in_=src[a].rearrange("p t i -> p (t i)").bitcast(I32))
+            return tile
+
+        def load_rows(src, a, cols, name):
+            tile = turn([P, 4, W], F32, "wide", 8, name)
+            nc.sync.dma_start(out=tile[:], in_=src[W * a : W * (a + 1), cols].rearrange("(p j) c -> p j c", j=4))
+            return tile
+
+        def quantize(grouped, name, late=False):
+            if late:
+                codes = turn([P, W], U32, "late_codes", 2, name + "_codes")
+                scales = turn([P, W], U8, "late_scales", 2, name + "_scales")
+            else:
+                codes = held([P, W], U32, name + "_codes")
+                scales = held([P, W], U8, name + "_scales")
+            nc.vector.quantize_mx(out=codes[:].bitcast(FP8X4), scales=scales[:], in_=grouped[:])
+            return codes, scales
+
+        def gather(window, offsets, dtype, name):
+            picked = held([P, W], dtype, name)
+            nc.vector.tensor_copy(picked[:], window.indirect(offsets))
+            return picked
+
+        tab_plane = load_scales(tab_scales, "tab_plane", nc.vector)
+        fill_scales(tab_plane, tab_scales, nc.scalar)
+        w2_plane = load_scales(w2_scales, "w2_plane", nc.vector)
+        tab2_plane = load_scales(tab2_scales, "tab2_plane", nc.vector)
+        w4_plane = load_scales(w4_scales, "w4_plane", nc.vector)
+        one = keep.tile([P, 1], F32, name="one")
+        quarter_pi = keep.tile([P, 1], F32, name="quarter_pi")
+        nc.vector.memset(one[:], 1.0)
+        nc.vector.tensor_scalar(quarter_pi[:], one[:], math.pi / 4, 0.0, ALU.mult, ALU.add)
+
+        idx = load_list(offs, "idx")
+        w2_raw = held([P, 2 * H], U8, "w2_raw")
+        nc.sync.dma_start(out=w2_raw[:].bitcast(I32), in_=w2_words[0].bitcast(I32))
+
+        w2_dealt = held([P, 2 * H], U8, "w2_dealt")
+        w2_dealt_plane = held([P, H], U8, "w2_dealt_plane")
+
+        def deal_w2_words(b):
+            nc.vector.tensor_copy(
+                out=w2_dealt[:, 2 * W * b : 2 * W * (b + 1)].rearrange("p (t m e) -> p t m e", t=4, e=2),
+                in_=w2_raw[:, 2 * W * b : 2 * W * (b + 1)].rearrange("p (m t e) -> p t m e", t=4, e=2),
+            )
+
+        def deal_w2_scales():
+            nc.vector.tensor_copy(
+                out=w2_dealt_plane[:].rearrange("p (b t m) -> p b t m", b=2, t=4),
+                in_=w2_plane[:].rearrange("p (b m t) -> p b t m", b=2, t=4),
+            )
+
+        def round_w1(raw, name, copy):
+            grouped = turn([P, 4 * W], BF16, "grouped", 4, name)
+            copy(
+                out=grouped[:].rearrange("p (t m j) -> p m j t", t=4, j=4),
+                in_=raw[:].rearrange("p j (m t) -> p m j t", t=4),
+            )
+            return grouped
+
+        deal_w2_words(0)
+        deal_w2_words(1)
+
+        w1_q = {}
+        v_words = {}
+        v_plane = {}
+        tab_tiles = [load_words(tab_words, 0, "tab_0")]
+        w1_raw = [load_rows(w1, a, slice(0, W), "w1_raw_%d_0" % a) for a in range(2)]
+        tab_tiles.append(load_words(tab_words, 1, "tab_1"))
+        w1_raw_late = [load_rows(w1, a, slice(W, 2 * W), "w1_raw_%d_1" % a) for a in range(2)]
+        p1 = load_list(pos1, "p1")
+        idx2 = load_list(offs2, "idx2")
+        fill_scales(tab2_plane, tab2_scales, nc.sync)
+        tab2_tile = load_words(tab2_words, 0, "tab2")
+        fill_scales(w2_plane, w2_scales, nc.sync)
+
+        def gather_words(a):
+            for ch in range(2):
+                v_words[a, ch] = gather(tab_tiles[a][:].bitcast(U32), idx[:, 32 * ch : 32 * ch + 32], U32, "v_words_%d_%d" % (a, ch))
+
+        gather_words(0)
+        for ch in range(2):
+            v_plane[ch] = gather(tab_plane[:], idx[:, 32 * ch : 32 * ch + 32], U8, "v_plane_%d" % ch)
+        for a in range(2):
+            w1_q[a, 0] = quantize(round_w1(w1_raw[a], "w1_grouped_%d_0" % a, nc.scalar.copy), "w1_%d_0" % a)
+        gather_words(1)
+        w1_q[0, 1] = quantize(round_w1(w1_raw_late[0], "w1_grouped_0_1", nc.vector.tensor_copy), "w1_0_1", True)
+        idx4 = load_list(offs4, "idx4")
+        w4_codes = held([P, 2, N], I32, "w4_codes")
+        nc.sync.dma_start(out=w4_codes[:], in_=w4_words.rearrange("a p c i -> p a (c i)").bitcast(I32))
+        fill_scales(w4_plane, w4_scales, nc.sync)
+        resid_tile = turn([P, 4, PK], F32, "wide", 8, "resid_tile")
+        nc.sync.dma_start(out=resid_tile[:], in_=resid.rearrange("(c p) j -> p c j", p=P))
+        wg2_tile = held([P, PK], F32, "wg2_tile")
+        nc.sync.dma_start(out=wg2_tile[:], in_=wg2)
+        gain_tile = held([P, 2, 4], F32, "gain_tile")
+        nc.sync.dma_start(out=gain_tile[:], in_=gain.rearrange("(b p t) -> p b t", b=2, t=4))
+
+        def load_page(c):
+            tile = turn([P, T], F32, "wide", 8, "page_%d" % c)
+            nc.sync.dma_start(out=tile[:], in_=page1[P * c : P * (c + 1), :])
+            return tile
+
+        pages = [load_page(0)]
+        w3_raw = [load_rows(w3, b, slice(0, N), "w3_raw_%d" % b) for b in range(2)]
+        pages.extend([load_page(c) for c in range(1, 4)])
+        idx3 = load_list(offs3, "idx3")
+        wg1_tile = held([P, S], F32, "wg1_tile")
+        nc.sync.dma_start(out=wg1_tile[:], in_=wg1)
+
+        h1 = {}
+
+        def first_stage(b, t):
+            cols = slice(P * t, P * (t + 1))
+            half_sine = held([P, S], F32, "h1_%d_%d" % (b, t))
+            for ch in range(2):
+                acc = psum.tile([P, W], F32, tag="x", bufs=4, name="x_%d_%d_%d" % (b, t, ch))
+                for a in range(2):
+                    codes, scales = w1_q[a, b]
+                    nc.tensor.matmul_mx(
+                        out=acc[:], lhsT=codes[:, cols].bitcast(FP8X4), lhsT_scale=scales[:, cols],
+                        rhs=v_words[a, ch][:].bitcast(FP8X4), rhs_scale=v_plane[ch][4 * a :, :],
+                        start=(a == 0), stop=(a == 1),
+                    )
+                nc.scalar.activation(half_sine[:, W * ch : W * (ch + 1)], acc[:], ACT.Sin, bias=quarter_pi[:], scale=-0.5)
+            nc.scalar.activation(half_sine[:], half_sine[:], ACT.Square)
+            nc.vector.tensor_scalar(half_sine[:], half_sine[:], -2.0, 1.0, ALU.mult, ALU.add)
+            h1[b, t] = half_sine
+
+        def woven(ap3):
+            return ap3.rearrange("p t (c i) -> p c t i", i=4)
+
+        def woven_out(grouped, cols):
+            return grouped[:].rearrange("p (j t) -> p j t", t=4)[:, cols, :].rearrange("p (c i) t -> p c t i", i=4)
+
+        def make_z2(b, picked):
+            grouped = turn([P, 4 * W], BF16, "grouped", 4, "z2_grouped_%d" % b)
+            for g in range(4):
+                cols = slice(P * g, P * (g + 1))
+                acc = psum.tile([P, 4, P], F32, tag="late", bufs=4, name="h2_%d_%d" % (b, g))
+                for t in range(4):
+                    r0 = W * b + P * t
+                    nc.tensor.matmul_mx(
+                        out=acc[:, t, :], lhsT=w2_dealt[:, 2 * r0 : 2 * (r0 + P)].bitcast(FP4X4),
+                        lhsT_scale=w2_dealt_plane[:, r0 : r0 + P],
+                        rhs=v2_words[:, cols].bitcast(FP8X4), rhs_scale=v2_plane[:, cols],
+                        start=True, stop=True,
+                    )
+                nc.vector.tensor_tensor(woven_out(grouped, cols), woven(acc[:]), woven(picked[:, :, cols]), ALU.mult)
+            return quantize(grouped, "z2_%d" % b)
+
+        z2_q = {}
+        picked = {b: turn([P, 4, PK], F32, "picked", 2, "picked_%d" % b) for b in range(2)}
+        for b in range(2):
+            for t in range(4):
+                first_stage(b, t)
+                if b == 0 and t == 1:
+                    grouped = round_w1(w1_raw_late[1], "w1_grouped_1_1", nc.scalar.copy)
+                if b == 0 and t == 2:
+                    w1_q[1, 1] = quantize(grouped, "w1_1_1", True)
+                nc.vector.tensor_copy(picked[b][:, t, :], h1[b, t][:].indirect(p1[:]))
+            if b == 0:
+                deal_w2_scales()
+                v2_words = gather(tab2_tile[:].bitcast(U32), idx2[:], U32, "v2_words")
+                v2_plane = gather(tab2_plane[:], idx2[:], U8, "v2_plane")
+            z2_q[b] = make_z2(b, picked[b])
+
+        def second_product(weights, moving, name):
+            acc = psum.tile([P, W], F32, tag="late", bufs=4, name=name)
+            for b in range(2):
+                w_codes, w_scales = weights[b]
+                codes, scales = moving[b]
+                nc.tensor.matmul_mx(
+                    out=acc[:], lhsT=w_codes.bitcast(FP8X4), lhsT_scale=w_scales,
+                    rhs=codes[:].bitcast(FP8X4), rhs_scale=scales[:], start=(b == 0), stop=(b == 1),
+                )
+            return acc
+
+        y2 = []
+        for c in range(4):
+            cols = slice(P * c, P * (c + 1))
+            acc = second_product([(w4_codes[:, b, cols], w4_plane[4 * b :, cols]) for b in range(2)], z2_q, "y2_%d" % c)
+            staged = turn([P, W], F32, "staged", 4, "y2_staged_%d" % c)
+            nc.vector.tensor_tensor(staged[:], acc[:], resid_tile[:, c, :], ALU.add)
+            y2.append(staged)
+            if c >= 1:
+                nc.vector.tensor_tensor(pages[c - 1][:].indirect(idx4[:]), y2[c - 1][:], wg2_tile[:], ALU.mult)
+        nc.vector.tensor_tensor(pages[3][:].indirect(idx4[:]), y2[3][:], wg2_tile[:], ALU.mult)
+
+        w3_q = {}
+        for b in range(2):
+            grouped = turn([P, 4 * W], BF16, "late_codes", 2, "w3_grouped_%d" % b)
+            nc.scalar.copy(out=woven_out(grouped, slice(0, W)), in_=woven(w3_raw[b][:]))
+            w3_q[b] = quantize(grouped, "w3_%d" % b)
+
+        for ch in range(2):
+            span = slice(W * ch, W * (ch + 1))
+            z1_q = {}
+            for b in range(2):
+                rounded = turn([P, 4, W], BF16, "late_scales", 2, "z1_rounded_%d_%d" % (ch, b))
+                for t in range(4):
+                    nc.scalar.activation(rounded[:, t, :], h1[b, t][:, span], ACT.Copy, scale=gain_tile[:, b, t : t + 1])
+                grouped = turn([P, 4 * W], BF16, "grouped", 4, "z1_grouped_%d_%d" % (ch, b))
+                nc.scalar.copy(out=woven_out(grouped, slice(0, W)), in_=woven(rounded[:]))
+                z1_q[b] = quantize(grouped, "z1_%d_%d" % (ch, b))
+            for c in range(4):
+                cols = slice(P * c, P * (c + 1))
+                acc = second_product([(w3_q[b][0][:, cols], w3_q[b][1][:, cols]) for b in range(2)], z1_q, "y1_%d_%d" % (ch, c))
+                staged = turn([P, W], F32, "staged", 4, "y1_staged_%d_%d" % (ch, c))
+                nc.scalar.copy(out=staged[:], in_=acc[:])
+                nc.vector.tensor_tensor(pages[c][:].indirect(idx3[:, 32 * ch : 32 * ch + 32]), staged[:], wg1_tile[:, span], ALU.mult)
+                if ch == 1:
+                    nc.sync.dma_start(out=out[P * c : P * (c + 1), :], in_=pages[c][:])

@@ -19,6 +19,7 @@ ACT = mybir.ActivationFunctionType
 
 P = 128
 W = 512
+ON_SCALAR = 0
 
 
 def tile_list_excursion_risk_slots_kernel(
@@ -29,6 +30,7 @@ def tile_list_excursion_risk_slots_kernel(
     with ExitStack() as ctx:
         keep = ctx.enter_context(tc.tile_pool(name="keep", bufs=1))
         ring = ctx.enter_context(tc.tile_pool(name="ring", bufs=2))
+        reuse = ctx.enter_context(tc.tile_pool(name="reuse", bufs=1))
         psum = ctx.enter_context(tc.psum_pool(name="psum", bufs=1))
 
         def held(shape, dtype, name):
@@ -56,47 +58,52 @@ def tile_list_excursion_risk_slots_kernel(
                     in_=src[:, 4 * q : 4 * q + 4, :].bitcast(I32),
                 )
 
-        def load_words(src, a, name):
-            tile = turn([P, T], I32, "wide", 8, name)
+        def load_words(src, a, name, offset=None):
+            if offset is None:
+                tile = turn([P, T], I32, "wide", 7, name)
+            else:
+                tile = reuse.tile([P, T], I32, name=name, align_bytes=64, offset=offset)
             nc.sync.dma_start(out=tile[:], in_=src[a].rearrange("p t i -> p (t i)").bitcast(I32))
             return tile
 
-        def load_rows(src, a, cols, name):
-            tile = turn([P, 4, W], F32, "wide", 8, name)
+        def load_rows(src, a, cols, name, offset=None):
+            if offset is None:
+                tile = turn([P, 4, W], F32, "wide", 7, name)
+            else:
+                tile = reuse.tile([P, 4, W], F32, name=name, align_bytes=64, offset=offset)
             nc.sync.dma_start(out=tile[:], in_=src[W * a : W * (a + 1), cols].rearrange("(p j) c -> p j c", j=4))
             return tile
 
-        def quantize(grouped, name, late=False):
-            if late:
-                codes = turn([P, W], U32, "late_codes", 2, name + "_codes")
-                scales = turn([P, W], U8, "late_scales", 2, name + "_scales")
-            else:
-                codes = held([P, W], U32, name + "_codes")
-                scales = held([P, W], U8, name + "_scales")
+        def quantize(grouped, name):
+            codes = held([P, W], U32, name + "_codes")
+            scales = held([P, W], U8, name + "_scales")
             nc.vector.quantize_mx(out=codes[:].bitcast(FP8X4), scales=scales[:], in_=grouped[:])
             return codes, scales
 
-        def gather(window, offsets, dtype, name):
-            picked = held([P, W], dtype, name)
+        def gather(window, offsets, dtype, name, offset=None):
+            if offset is None:
+                picked = held([P, W], dtype, name)
+            else:
+                picked = reuse.tile([P, W], dtype, name=name, align_bytes=64, offset=offset)
             nc.vector.tensor_copy(picked[:], window.indirect(offsets))
             return picked
 
         tab_plane = load_scales(tab_scales, "tab_plane", nc.vector)
-        fill_scales(tab_plane, tab_scales, nc.scalar)
-        w2_plane = load_scales(w2_scales, "w2_plane", nc.vector)
-        tab2_plane = load_scales(tab2_scales, "tab2_plane", nc.vector)
-        w4_plane = load_scales(w4_scales, "w4_plane", nc.vector)
-        one = keep.tile([P, 1], F32, name="one")
+        w2_plane = load_scales(w2_scales, "w2_plane", nc.gpsimd)
+        tab2_plane = load_scales(tab2_scales, "tab2_plane", nc.gpsimd)
+        w4_plane = load_scales(w4_scales, "w4_plane", nc.gpsimd)
+        zero = keep.tile([P, 1], F32, name="zero")
+        sine_of_zero = keep.tile([P, 1], F32, name="sine_of_zero")
         quarter_pi = keep.tile([P, 1], F32, name="quarter_pi")
-        nc.vector.memset(one[:], 1.0)
-        nc.vector.tensor_scalar(quarter_pi[:], one[:], math.pi / 4, 0.0, ALU.mult, ALU.add)
+        nc.gpsimd.memset(zero[:], 0.0)
+        nc.scalar.activation(sine_of_zero[:], zero[:], ACT.Sin)
+        nc.gpsimd.tensor_scalar(quarter_pi[:], sine_of_zero[:], 1.0, math.pi / 4, ALU.mult, ALU.add)
 
         idx = load_list(offs, "idx")
         w2_raw = held([P, 2 * H], U8, "w2_raw")
         nc.sync.dma_start(out=w2_raw[:].bitcast(I32), in_=w2_words[0].bitcast(I32))
 
         w2_dealt = held([P, 2 * H], U8, "w2_dealt")
-        w2_dealt_plane = held([P, H], U8, "w2_dealt_plane")
 
         def deal_w2_words(b):
             nc.vector.tensor_copy(
@@ -111,11 +118,15 @@ def tile_list_excursion_risk_slots_kernel(
             )
 
         def round_w1(raw, name, copy):
-            grouped = turn([P, 4 * W], BF16, "grouped", 4, name)
-            copy(
-                out=grouped[:].rearrange("p (t m j) -> p m j t", t=4, j=4),
-                in_=raw[:].rearrange("p j (m t) -> p m j t", t=4),
-            )
+            if name == "w1_grouped_1_0":
+                grouped = reuse.tile([P, 4 * W], BF16, name=name, align_bytes=64, offset=0)
+            else:
+                grouped = turn([P, 4 * W], BF16, "grouped", 4, name)
+            for part, (m0, m1) in zip(copy, ((0, 80), (80, P)) if len(copy) == 2 else ((0, P),)):
+                part(
+                    out=grouped[:].rearrange("p (t m j) -> p m j t", t=4, j=4)[:, m0:m1],
+                    in_=raw[:].rearrange("p j (m t) -> p m j t", t=4)[:, m0:m1],
+                )
             return grouped
 
         deal_w2_words(0)
@@ -125,31 +136,35 @@ def tile_list_excursion_risk_slots_kernel(
         v_words = {}
         v_plane = {}
         tab_tiles = [load_words(tab_words, 0, "tab_0")]
+        fill_scales(tab_plane, tab_scales, nc.sync)
         w1_raw = [load_rows(w1, a, slice(0, W), "w1_raw_%d_0" % a) for a in range(2)]
-        tab_tiles.append(load_words(tab_words, 1, "tab_1"))
-        w1_raw_late = [load_rows(w1, a, slice(W, 2 * W), "w1_raw_%d_1" % a) for a in range(2)]
-        p1 = load_list(pos1, "p1")
-        idx2 = load_list(offs2, "idx2")
-        fill_scales(tab2_plane, tab2_scales, nc.sync)
-        tab2_tile = load_words(tab2_words, 0, "tab2")
+        tab_tiles.append(load_words(tab_words, 1, "tab_1", 4096))
         fill_scales(w2_plane, w2_scales, nc.sync)
+        idx2 = load_list(offs2, "idx2")
+        tab2_tile = load_words(tab2_words, 0, "tab2")
+        fill_scales(tab2_plane, tab2_scales, nc.sync)
+        p1 = load_list(pos1, "p1")
+        w1_raw_late = [load_rows(w1, a, slice(W, 2 * W), "w1_raw_%d_1" % a) for a in range(2)]
 
         def gather_words(a):
             for ch in range(2):
-                v_words[a, ch] = gather(tab_tiles[a][:].bitcast(U32), idx[:, 32 * ch : 32 * ch + 32], U32, "v_words_%d_%d" % (a, ch))
+                v_words[a, ch] = gather(tab_tiles[a][:].bitcast(U32), idx[:, 32 * ch : 32 * ch + 32], U32, "v_words_%d_%d" % (a, ch), 2048 * ch if a else None)
 
         gather_words(0)
         for ch in range(2):
             v_plane[ch] = gather(tab_plane[:], idx[:, 32 * ch : 32 * ch + 32], U8, "v_plane_%d" % ch)
         for a in range(2):
-            w1_q[a, 0] = quantize(round_w1(w1_raw[a], "w1_grouped_%d_0" % a, nc.scalar.copy), "w1_%d_0" % a)
+            w1_q[a, 0] = quantize(round_w1(w1_raw[a], "w1_grouped_%d_0" % a, [nc.scalar.copy, nc.vector.tensor_copy][: a + 1]), "w1_%d_0" % a)
         gather_words(1)
-        w1_q[0, 1] = quantize(round_w1(w1_raw_late[0], "w1_grouped_0_1", nc.vector.tensor_copy), "w1_0_1", True)
+        w2_dealt_plane = reuse.tile([P, H], U8, name="w2_dealt_plane", align_bytes=64, offset=6656)
+        deal_w2_scales()
+        v2_words = gather(tab2_tile[:].bitcast(U32), idx2[:], U32, "v2_words", 4096)
+        v2_plane = gather(tab2_plane[:], idx2[:], U8, "v2_plane", 6144)
         idx4 = load_list(offs4, "idx4")
         w4_codes = held([P, 2, N], I32, "w4_codes")
         nc.sync.dma_start(out=w4_codes[:], in_=w4_words.rearrange("a p c i -> p a (c i)").bitcast(I32))
         fill_scales(w4_plane, w4_scales, nc.sync)
-        resid_tile = turn([P, 4, PK], F32, "wide", 8, "resid_tile")
+        resid_tile = turn([P, 4, PK], F32, "wide", 7, "resid_tile")
         nc.sync.dma_start(out=resid_tile[:], in_=resid.rearrange("(c p) j -> p c j", p=P))
         wg2_tile = held([P, PK], F32, "wg2_tile")
         nc.sync.dma_start(out=wg2_tile[:], in_=wg2)
@@ -157,35 +172,45 @@ def tile_list_excursion_risk_slots_kernel(
         nc.sync.dma_start(out=gain_tile[:], in_=gain.rearrange("(b p t) -> p b t", b=2, t=4))
 
         def load_page(c):
-            tile = turn([P, T], F32, "wide", 8, "page_%d" % c)
+            tile = turn([P, T], F32, "wide", 7, "page_%d" % c)
             nc.sync.dma_start(out=tile[:], in_=page1[P * c : P * (c + 1), :])
             return tile
 
         pages = [load_page(0)]
-        w3_raw = [load_rows(w3, b, slice(0, N), "w3_raw_%d" % b) for b in range(2)]
+        w3_raw = [load_rows(w3, b, slice(0, N), "w3_raw_%d" % b, 12288 if b else None) for b in range(2)]
         pages.extend([load_page(c) for c in range(1, 4)])
         idx3 = load_list(offs3, "idx3")
         wg1_tile = held([P, S], F32, "wg1_tile")
         nc.sync.dma_start(out=wg1_tile[:], in_=wg1)
 
         h1 = {}
+        sines = {}
 
-        def first_stage(b, t):
+        def half_sine(b, t, ch):
             cols = slice(P * t, P * (t + 1))
-            half_sine = held([P, S], F32, "h1_%d_%d" % (b, t))
-            for ch in range(2):
-                acc = psum.tile([P, W], F32, tag="x", bufs=4, name="x_%d_%d_%d" % (b, t, ch))
-                for a in range(2):
-                    codes, scales = w1_q[a, b]
-                    nc.tensor.matmul_mx(
-                        out=acc[:], lhsT=codes[:, cols].bitcast(FP8X4), lhsT_scale=scales[:, cols],
-                        rhs=v_words[a, ch][:].bitcast(FP8X4), rhs_scale=v_plane[ch][4 * a :, :],
-                        start=(a == 0), stop=(a == 1),
-                    )
-                nc.scalar.activation(half_sine[:, W * ch : W * (ch + 1)], acc[:], ACT.Sin, bias=quarter_pi[:], scale=-0.5)
-            nc.scalar.activation(half_sine[:], half_sine[:], ACT.Square)
-            nc.vector.tensor_scalar(half_sine[:], half_sine[:], -2.0, 1.0, ALU.mult, ALU.add)
-            h1[b, t] = half_sine
+            if ch == 0:
+                h1[b, t] = held([P, S], F32, "h1_%d_%d" % (b, t))
+                sines[b, t] = h1[b, t]
+                if (b, t) == (1, 3):
+                    sines[b, t] = reuse.tile([P, S], F32, name="last_sine", align_bytes=64, offset=22528)
+            acc = psum.tile([P, W], F32, tag="x", bufs=4, name="x_%d_%d_%d" % (b, t, ch))
+            for a in range(2):
+                codes, scales = w1_q[a, b]
+                nc.tensor.matmul_mx(
+                    out=acc[:], lhsT=codes[:, cols].bitcast(FP8X4), lhsT_scale=scales[:, cols],
+                    rhs=v_words[a, ch][:].bitcast(FP8X4), rhs_scale=v_plane[ch][4 * a :, :],
+                    start=(a == 0), stop=(a == 1),
+                )
+            nc.scalar.activation(sines[b, t][:, W * ch : W * (ch + 1)], acc[:], ACT.Sin, bias=quarter_pi[:], scale=-0.5)
+
+        def square(b, t):
+            nc.scalar.activation(h1[b, t][:], sines[b, t][:], ACT.Square)
+
+        def finish_sine(b, t):
+            if b == 0 and t < ON_SCALAR:
+                nc.scalar.activation(h1[b, t][:], h1[b, t][:], ACT.Copy, bias=1.0, scale=-2.0)
+            else:
+                nc.gpsimd.tensor_scalar(h1[b, t][:], h1[b, t][:], -2.0, 1.0, ALU.mult, ALU.add)
 
         def woven(ap3):
             return ap3.rearrange("p t (c i) -> p c t i", i=4)
@@ -197,7 +222,7 @@ def tile_list_excursion_risk_slots_kernel(
             grouped = turn([P, 4 * W], BF16, "grouped", 4, "z2_grouped_%d" % b)
             for g in range(4):
                 cols = slice(P * g, P * (g + 1))
-                acc = psum.tile([P, 4, P], F32, tag="late", bufs=4, name="h2_%d_%d" % (b, g))
+                acc = psum.tile([P, 4, P], F32, tag="x" if b else "late", bufs=4, name="h2_%d_%d" % (b, g))
                 for t in range(4):
                     r0 = W * b + P * t
                     nc.tensor.matmul_mx(
@@ -211,18 +236,22 @@ def tile_list_excursion_risk_slots_kernel(
 
         z2_q = {}
         picked = {b: turn([P, 4, PK], F32, "picked", 2, "picked_%d" % b) for b in range(2)}
+        half_sine(0, 0, 0)
         for b in range(2):
             for t in range(4):
-                first_stage(b, t)
-                if b == 0 and t == 1:
-                    grouped = round_w1(w1_raw_late[1], "w1_grouped_1_1", nc.scalar.copy)
-                if b == 0 and t == 2:
-                    w1_q[1, 1] = quantize(grouped, "w1_1_1", True)
+                half_sine(b, t, 1)
+                if t < 3 or b == 0:
+                    if t == 3:
+                        half_sine(1, 0, 0)
+                    else:
+                        half_sine(b, t + 1, 0)
+                square(b, t)
+                finish_sine(b, t)
+                if b == 0 and t < 2:
+                    grouped = round_w1(w1_raw_late[t], "w1_grouped_%d_1" % t, [nc.vector.tensor_copy])
                 nc.vector.tensor_copy(picked[b][:, t, :], h1[b, t][:].indirect(p1[:]))
-            if b == 0:
-                deal_w2_scales()
-                v2_words = gather(tab2_tile[:].bitcast(U32), idx2[:], U32, "v2_words")
-                v2_plane = gather(tab2_plane[:], idx2[:], U8, "v2_plane")
+                if b == 0 and t < 2:
+                    w1_q[t, 1] = quantize(grouped, "w1_%d_1" % t)
             z2_q[b] = make_z2(b, picked[b])
 
         def second_product(weights, moving, name):
@@ -236,38 +265,52 @@ def tile_list_excursion_risk_slots_kernel(
                 )
             return acc
 
-        y2 = []
-        for c in range(4):
+        def put(c, offsets, staged, weight):
+            nc.vector.tensor_tensor(pages[c][:].indirect(offsets), staged[:], weight, ALU.mult)
+
+        def stage_y2(c, staged):
             cols = slice(P * c, P * (c + 1))
             acc = second_product([(w4_codes[:, b, cols], w4_plane[4 * b :, cols]) for b in range(2)], z2_q, "y2_%d" % c)
-            staged = turn([P, W], F32, "staged", 4, "y2_staged_%d" % c)
             nc.vector.tensor_tensor(staged[:], acc[:], resid_tile[:, c, :], ALU.add)
-            y2.append(staged)
-            if c >= 1:
-                nc.vector.tensor_tensor(pages[c - 1][:].indirect(idx4[:]), y2[c - 1][:], wg2_tile[:], ALU.mult)
-        nc.vector.tensor_tensor(pages[3][:].indirect(idx4[:]), y2[3][:], wg2_tile[:], ALU.mult)
+            return staged
+
+        def stage_y1(ch, c, staged):
+            cols = slice(P * c, P * (c + 1))
+            acc = second_product([(w3_q[b][0][:, cols], w3_q[b][1][:, cols]) for b in range(2)], z1_q[ch], "y1_%d_%d" % (ch, c))
+            nc.scalar.copy(out=staged[:], in_=acc[:])
+            return staged
+
+        def make_z1(ch):
+            span = slice(W * ch, W * (ch + 1))
+            made = {}
+            for b in range(2):
+                rounded = reuse.tile([P, 4, W], BF16, name="z1_rounded_%d_%d" % (ch, b), align_bytes=64, offset=12288 + 4096 * b)
+                for t in range(4):
+                    nc.scalar.activation(rounded[:, t, :], h1[b, t][:, span], ACT.Copy, scale=gain_tile[:, b, t : t + 1])
+                if b == 0:
+                    grouped = turn([P, 4 * W], BF16, "grouped", 4, "z1_grouped_%d_%d" % (ch, b))
+                else:
+                    grouped = turn([P, 4 * W], BF16, "last_%d" % ch, 1, "z1_grouped_%d_%d" % (ch, b))
+                nc.scalar.copy(out=woven_out(grouped, slice(0, W)), in_=woven(rounded[:]))
+                made[b] = quantize(grouped, "z1_%d_%d" % (ch, b))
+            return made
+
+        y2 = [stage_y2(c, turn([P, W], F32, "staged", 4, "y2_staged_%d" % c)) for c in range(3)]
+        for c in range(3):
+            put(c, idx4[:], y2[c], wg2_tile[:])
 
         w3_q = {}
         for b in range(2):
-            grouped = turn([P, 4 * W], BF16, "late_codes", 2, "w3_grouped_%d" % b)
+            grouped = reuse.tile([P, 4 * W], BF16, name="w3_grouped_%d" % b, align_bytes=64, offset=20480 + 4096 * b)
             nc.scalar.copy(out=woven_out(grouped, slice(0, W)), in_=woven(w3_raw[b][:]))
             w3_q[b] = quantize(grouped, "w3_%d" % b)
 
-        for ch in range(2):
-            span = slice(W * ch, W * (ch + 1))
-            z1_q = {}
-            for b in range(2):
-                rounded = turn([P, 4, W], BF16, "late_scales", 2, "z1_rounded_%d_%d" % (ch, b))
-                for t in range(4):
-                    nc.scalar.activation(rounded[:, t, :], h1[b, t][:, span], ACT.Copy, scale=gain_tile[:, b, t : t + 1])
-                grouped = turn([P, 4 * W], BF16, "grouped", 4, "z1_grouped_%d_%d" % (ch, b))
-                nc.scalar.copy(out=woven_out(grouped, slice(0, W)), in_=woven(rounded[:]))
-                z1_q[b] = quantize(grouped, "z1_%d_%d" % (ch, b))
-            for c in range(4):
-                cols = slice(P * c, P * (c + 1))
-                acc = second_product([(w3_q[b][0][:, cols], w3_q[b][1][:, cols]) for b in range(2)], z1_q, "y1_%d_%d" % (ch, c))
-                staged = turn([P, W], F32, "staged", 4, "y1_staged_%d_%d" % (ch, c))
-                nc.scalar.copy(out=staged[:], in_=acc[:])
-                nc.vector.tensor_tensor(pages[c][:].indirect(idx3[:, 32 * ch : 32 * ch + 32]), staged[:], wg1_tile[:, span], ALU.mult)
-                if ch == 1:
-                    nc.sync.dma_start(out=out[P * c : P * (c + 1), :], in_=pages[c][:])
+        z1_q = {0: make_z1(0)}
+        put(3, idx4[:], stage_y2(3, turn([P, W], F32, "last_0", 1, "y2_staged_3")), wg2_tile[:])
+        for c in range(3):
+            put(c, idx3[:, 0:32], stage_y1(0, c, turn([P, W], F32, "staged", 4, "y1_staged_0_%d" % c)), wg1_tile[:, 0:W])
+        z1_q[1] = make_z1(1)
+        put(3, idx3[:, 0:32], stage_y1(0, 3, turn([P, W], F32, "last_1", 1, "y1_staged_0_3")), wg1_tile[:, 0:W])
+        for c in range(4):
+            put(c, idx3[:, 32:64], stage_y1(1, c, turn([P, W], F32, "staged", 4, "y1_staged_1_%d" % c)), wg1_tile[:, W : 2 * W])
+            nc.sync.dma_start(out=out[P * c : P * (c + 1), :], in_=pages[c][:])

@@ -118,10 +118,11 @@ def tile_list_excursion_risk_slots_kernel(
             )
 
         def round_w1(raw, name, copy):
-            if name == "w1_grouped_1_0":
-                grouped = reuse.tile([P, 4 * W], BF16, name=name, align_bytes=64, offset=0)
+            places = {"w1_grouped_1_0": 0, "w1_grouped_0_1": 28672, "w1_grouped_1_1": 32768}
+            if name in places:
+                grouped = reuse.tile([P, 4 * W], BF16, name=name, align_bytes=64, offset=places[name])
             else:
-                grouped = turn([P, 4 * W], BF16, "grouped", 4, name)
+                grouped = turn([P, 4 * W], BF16, "grouped", 3, name)
             for part, (m0, m1) in zip(copy, ((0, 80), (80, P)) if len(copy) == 2 else ((0, P),)):
                 part(
                     out=grouped[:].rearrange("p (t m j) -> p m j t", t=4, j=4)[:, m0:m1],
@@ -219,7 +220,7 @@ def tile_list_excursion_risk_slots_kernel(
             return grouped[:].rearrange("p (j t) -> p j t", t=4)[:, cols, :].rearrange("p (c i) t -> p c t i", i=4)
 
         def make_z2(b, picked):
-            grouped = turn([P, 4 * W], BF16, "grouped", 4, "z2_grouped_%d" % b)
+            grouped = turn([P, 4 * W], BF16, "grouped", 3, "z2_grouped_%d" % b)
             for g in range(4):
                 cols = slice(P * g, P * (g + 1))
                 acc = psum.tile([P, 4, P], F32, tag="x" if b else "late", bufs=4, name="h2_%d_%d" % (b, g))
@@ -235,7 +236,9 @@ def tile_list_excursion_risk_slots_kernel(
             return quantize(grouped, "z2_%d" % b)
 
         z2_q = {}
-        picked = {b: turn([P, 4, PK], F32, "picked", 2, "picked_%d" % b) for b in range(2)}
+        for a in range(2):
+            w1_q[a, 1] = quantize(round_w1(w1_raw_late[a], "w1_grouped_%d_1" % a, [nc.vector.tensor_copy]), "w1_%d_1" % a)
+        picked = {0: reuse.tile([P, 4, PK], F32, name="picked_0", align_bytes=64, offset=28672), 1: held([P, 4, PK], F32, "picked_1")}
         half_sine(0, 0, 0)
         for b in range(2):
             for t in range(4):
@@ -247,11 +250,7 @@ def tile_list_excursion_risk_slots_kernel(
                         half_sine(b, t + 1, 0)
                 square(b, t)
                 finish_sine(b, t)
-                if b == 0 and t < 2:
-                    grouped = round_w1(w1_raw_late[t], "w1_grouped_%d_1" % t, [nc.vector.tensor_copy])
                 nc.vector.tensor_copy(picked[b][:, t, :], h1[b, t][:].indirect(p1[:]))
-                if b == 0 and t < 2:
-                    w1_q[t, 1] = quantize(grouped, "w1_%d_1" % t)
             z2_q[b] = make_z2(b, picked[b])
 
         def second_product(weights, moving, name):
@@ -288,7 +287,7 @@ def tile_list_excursion_risk_slots_kernel(
                 for t in range(4):
                     nc.scalar.activation(rounded[:, t, :], h1[b, t][:, span], ACT.Copy, scale=gain_tile[:, b, t : t + 1])
                 if b == 0:
-                    grouped = turn([P, 4 * W], BF16, "grouped", 4, "z1_grouped_%d_%d" % (ch, b))
+                    grouped = turn([P, 4 * W], BF16, "grouped", 3, "z1_grouped_%d_%d" % (ch, b))
                 else:
                     grouped = turn([P, 4 * W], BF16, "last_%d" % ch, 1, "z1_grouped_%d_%d" % (ch, b))
                 nc.scalar.copy(out=woven_out(grouped, slice(0, W)), in_=woven(rounded[:]))

@@ -19,7 +19,20 @@ ACT = mybir.ActivationFunctionType
 
 P = 128
 W = 512
-ON_SCALAR = 0
+LIST_COLUMNS = W // 16
+WIDE_BUFS = 7
+GROUPED_BUFS = 3
+STAGED_BUFS = 4
+BANKS = 4
+SCALAR_SHARE = 80
+AFFINE_ON_SCALAR = 2
+
+AT_W1_FIRST = 0
+AT_TAB = 4096
+AT_W3_RAW = 12288
+AT_W3_GROUPED = 20480
+AT_LAST_SINE = AT_W3_GROUPED + 2048
+AT_W1_SECOND = 28672
 
 
 def tile_list_excursion_risk_slots_kernel(
@@ -39,39 +52,38 @@ def tile_list_excursion_risk_slots_kernel(
         def turn(shape, dtype, tag, bufs, name):
             return ring.tile(shape, dtype, tag=tag, bufs=bufs, name=name, align_bytes=64)
 
+        def placed(shape, dtype, offset, name):
+            return reuse.tile(shape, dtype, name=name, align_bytes=64, offset=offset)
+
+        def wide(shape, dtype, name):
+            return turn(shape, dtype, "wide", WIDE_BUFS, name)
+
+        def entries(offsets, half):
+            return offsets[:, LIST_COLUMNS * half : LIST_COLUMNS * (half + 1)]
+
         def load_list(src, name):
             tile = keep.tile(list(src.shape), U16, name=name)
             nc.sync.dma_start(tile[:], src)
             return tile
 
-        def load_scales(src, name, engine):
-            passes, rows, width = src.shape
-            plane = held([P, width], U8, name)
+        def zeroed_plane(src, name, engine):
+            plane = held([P, src.shape[2]], U8, name)
             engine.memset(plane[:].bitcast(I32), 0)
             return plane
 
-        def fill_scales(plane, src, queue):
-            passes = src.shape[0]
+        def load_plane(plane, src):
             for q in range(4):
-                queue.dma_start(
-                    out=plane[32 * q : 32 * q + 4 * passes, :].bitcast(I32),
+                nc.sync.dma_start(
+                    out=plane[32 * q : 32 * q + 4 * src.shape[0], :].bitcast(I32),
                     in_=src[:, 4 * q : 4 * q + 4, :].bitcast(I32),
                 )
 
-        def load_words(src, a, name, offset=None):
-            if offset is None:
-                tile = turn([P, T], I32, "wide", 7, name)
-            else:
-                tile = reuse.tile([P, T], I32, name=name, align_bytes=64, offset=offset)
-            nc.sync.dma_start(out=tile[:], in_=src[a].rearrange("p t i -> p (t i)").bitcast(I32))
+        def load_words(tile, src):
+            nc.sync.dma_start(out=tile[:], in_=src.rearrange("p t i -> p (t i)").bitcast(I32))
             return tile
 
-        def load_rows(src, a, cols, name, offset=None):
-            if offset is None:
-                tile = turn([P, 4, W], F32, "wide", 7, name)
-            else:
-                tile = reuse.tile([P, 4, W], F32, name=name, align_bytes=64, offset=offset)
-            nc.sync.dma_start(out=tile[:], in_=src[W * a : W * (a + 1), cols].rearrange("(p j) c -> p j c", j=4))
+        def load_rows(tile, src):
+            nc.sync.dma_start(out=tile[:], in_=src.rearrange("(p j) c -> p j c", j=4))
             return tile
 
         def quantize(grouped, name):
@@ -80,18 +92,15 @@ def tile_list_excursion_risk_slots_kernel(
             nc.vector.quantize_mx(out=codes[:].bitcast(FP8X4), scales=scales[:], in_=grouped[:])
             return codes, scales
 
-        def gather(window, offsets, dtype, name, offset=None):
-            if offset is None:
-                picked = held([P, W], dtype, name)
-            else:
-                picked = reuse.tile([P, W], dtype, name=name, align_bytes=64, offset=offset)
-            nc.vector.tensor_copy(picked[:], window.indirect(offsets))
-            return picked
+        def gather(into, window, offsets):
+            nc.vector.tensor_copy(into[:], window.indirect(offsets))
+            return into
 
-        tab_plane = load_scales(tab_scales, "tab_plane", nc.vector)
-        w2_plane = load_scales(w2_scales, "w2_plane", nc.gpsimd)
-        tab2_plane = load_scales(tab2_scales, "tab2_plane", nc.gpsimd)
-        w4_plane = load_scales(w4_scales, "w4_plane", nc.gpsimd)
+        tab_plane = zeroed_plane(tab_scales, "tab_plane", nc.vector)
+        w2_plane = zeroed_plane(w2_scales, "w2_plane", nc.gpsimd)
+        tab2_plane = zeroed_plane(tab2_scales, "tab2_plane", nc.gpsimd)
+        w4_plane = zeroed_plane(w4_scales, "w4_plane", nc.gpsimd)
+
         zero = keep.tile([P, 1], F32, name="zero")
         sine_of_zero = keep.tile([P, 1], F32, name="sine_of_zero")
         quarter_pi = keep.tile([P, 1], F32, name="quarter_pi")
@@ -102,70 +111,67 @@ def tile_list_excursion_risk_slots_kernel(
         idx = load_list(offs, "idx")
         w2_raw = held([P, 2 * H], U8, "w2_raw")
         nc.sync.dma_start(out=w2_raw[:].bitcast(I32), in_=w2_words[0].bitcast(I32))
-
         w2_dealt = held([P, 2 * H], U8, "w2_dealt")
-
-        def deal_w2_words(b):
+        for b in range(2):
             nc.vector.tensor_copy(
                 out=w2_dealt[:, 2 * W * b : 2 * W * (b + 1)].rearrange("p (t m e) -> p t m e", t=4, e=2),
                 in_=w2_raw[:, 2 * W * b : 2 * W * (b + 1)].rearrange("p (m t e) -> p t m e", t=4, e=2),
             )
 
-        def deal_w2_scales():
-            nc.vector.tensor_copy(
-                out=w2_dealt_plane[:].rearrange("p (b t m) -> p b t m", b=2, t=4),
-                in_=w2_plane[:].rearrange("p (b m t) -> p b t m", b=2, t=4),
+        def load_w1(a, b):
+            tile = wide([P, 4, W], F32, "w1_raw_%d_%d" % (a, b))
+            return load_rows(tile, w1[W * a : W * (a + 1), W * b : W * (b + 1)])
+
+        tab_tiles = [load_words(wide([P, T], I32, "tab_0"), tab_words[0])]
+        load_plane(tab_plane, tab_scales)
+        w1_raw = {(a, 0): load_w1(a, 0) for a in range(2)}
+        tab_tiles.append(load_words(placed([P, T], I32, AT_TAB, "tab_1"), tab_words[1]))
+        load_plane(w2_plane, w2_scales)
+        idx2 = load_list(offs2, "idx2")
+        tab2_tile = load_words(wide([P, T], I32, "tab2"), tab2_words[0])
+        load_plane(tab2_plane, tab2_scales)
+        p1 = load_list(pos1, "p1")
+        for a in range(2):
+            w1_raw[a, 1] = load_w1(a, 1)
+
+        def round_w1(copy, grouped, raw, m0, m1):
+            copy(
+                out=grouped[:].rearrange("p (t m j) -> p m j t", t=4, j=4)[:, m0:m1],
+                in_=raw[:].rearrange("p j (m t) -> p m j t", t=4)[:, m0:m1],
             )
 
-        def round_w1(raw, name, copy):
-            places = {"w1_grouped_1_0": 0, "w1_grouped_0_1": 28672, "w1_grouped_1_1": 32768}
-            if name in places:
-                grouped = reuse.tile([P, 4 * W], BF16, name=name, align_bytes=64, offset=places[name])
-            else:
-                grouped = turn([P, 4 * W], BF16, "grouped", 3, name)
-            for part, (m0, m1) in zip(copy, ((0, 80), (80, P)) if len(copy) == 2 else ((0, P),)):
-                part(
-                    out=grouped[:].rearrange("p (t m j) -> p m j t", t=4, j=4)[:, m0:m1],
-                    in_=raw[:].rearrange("p j (m t) -> p m j t", t=4)[:, m0:m1],
-                )
-            return grouped
-
-        deal_w2_words(0)
-        deal_w2_words(1)
-
-        w1_q = {}
         v_words = {}
         v_plane = {}
-        tab_tiles = [load_words(tab_words, 0, "tab_0")]
-        fill_scales(tab_plane, tab_scales, nc.sync)
-        w1_raw = [load_rows(w1, a, slice(0, W), "w1_raw_%d_0" % a) for a in range(2)]
-        tab_tiles.append(load_words(tab_words, 1, "tab_1", 4096))
-        fill_scales(w2_plane, w2_scales, nc.sync)
-        idx2 = load_list(offs2, "idx2")
-        tab2_tile = load_words(tab2_words, 0, "tab2")
-        fill_scales(tab2_plane, tab2_scales, nc.sync)
-        p1 = load_list(pos1, "p1")
-        w1_raw_late = [load_rows(w1, a, slice(W, 2 * W), "w1_raw_%d_1" % a) for a in range(2)]
+        w1_q = {}
+        for half in range(2):
+            into = held([P, W], U32, "v_words_0_%d" % half)
+            v_words[0, half] = gather(into, tab_tiles[0][:].bitcast(U32), entries(idx, half))
+        for half in range(2):
+            v_plane[half] = gather(held([P, W], U8, "v_plane_%d" % half), tab_plane[:], entries(idx, half))
+        grouped = turn([P, 4 * W], BF16, "grouped", GROUPED_BUFS, "w1_grouped_0_0")
+        round_w1(nc.scalar.copy, grouped, w1_raw[0, 0], 0, P)
+        w1_q[0, 0] = quantize(grouped, "w1_0_0")
+        grouped = placed([P, 4 * W], BF16, AT_W1_FIRST, "w1_grouped_1_0")
+        round_w1(nc.scalar.copy, grouped, w1_raw[1, 0], 0, SCALAR_SHARE)
+        round_w1(nc.vector.tensor_copy, grouped, w1_raw[1, 0], SCALAR_SHARE, P)
+        w1_q[1, 0] = quantize(grouped, "w1_1_0")
+        for half in range(2):
+            into = placed([P, W], U32, AT_W1_FIRST + 4 * W * half, "v_words_1_%d" % half)
+            v_words[1, half] = gather(into, tab_tiles[1][:].bitcast(U32), entries(idx, half))
 
-        def gather_words(a):
-            for ch in range(2):
-                v_words[a, ch] = gather(tab_tiles[a][:].bitcast(U32), idx[:, 32 * ch : 32 * ch + 32], U32, "v_words_%d_%d" % (a, ch), 2048 * ch if a else None)
+        w2_dealt_plane = placed([P, H], U8, AT_TAB + 5 * W, "w2_dealt_plane")
+        nc.vector.tensor_copy(
+            out=w2_dealt_plane[:].rearrange("p (b t m) -> p b t m", b=2, t=4),
+            in_=w2_plane[:].rearrange("p (b m t) -> p b t m", b=2, t=4),
+        )
+        v2_words = gather(placed([P, PK], U32, AT_TAB, "v2_words"), tab2_tile[:].bitcast(U32), idx2[:])
+        v2_plane = gather(placed([P, PK], U8, AT_TAB + 4 * W, "v2_plane"), tab2_plane[:], idx2[:])
 
-        gather_words(0)
-        for ch in range(2):
-            v_plane[ch] = gather(tab_plane[:], idx[:, 32 * ch : 32 * ch + 32], U8, "v_plane_%d" % ch)
-        for a in range(2):
-            w1_q[a, 0] = quantize(round_w1(w1_raw[a], "w1_grouped_%d_0" % a, [nc.scalar.copy, nc.vector.tensor_copy][: a + 1]), "w1_%d_0" % a)
-        gather_words(1)
-        w2_dealt_plane = reuse.tile([P, H], U8, name="w2_dealt_plane", align_bytes=64, offset=6656)
-        deal_w2_scales()
-        v2_words = gather(tab2_tile[:].bitcast(U32), idx2[:], U32, "v2_words", 4096)
-        v2_plane = gather(tab2_plane[:], idx2[:], U8, "v2_plane", 6144)
         idx4 = load_list(offs4, "idx4")
         w4_codes = held([P, 2, N], I32, "w4_codes")
         nc.sync.dma_start(out=w4_codes[:], in_=w4_words.rearrange("a p c i -> p a (c i)").bitcast(I32))
-        fill_scales(w4_plane, w4_scales, nc.sync)
-        resid_tile = turn([P, 4, PK], F32, "wide", 7, "resid_tile")
+        load_plane(w4_plane, w4_scales)
+        resid_tile = wide([P, 4, PK], F32, "resid_tile")
         nc.sync.dma_start(out=resid_tile[:], in_=resid.rearrange("(c p) j -> p c j", p=P))
         wg2_tile = held([P, PK], F32, "wg2_tile")
         nc.sync.dma_start(out=wg2_tile[:], in_=wg2)
@@ -173,88 +179,90 @@ def tile_list_excursion_risk_slots_kernel(
         nc.sync.dma_start(out=gain_tile[:], in_=gain.rearrange("(b p t) -> p b t", b=2, t=4))
 
         def load_page(c):
-            tile = turn([P, T], F32, "wide", 7, "page_%d" % c)
+            tile = wide([P, T], F32, "page_%d" % c)
             nc.sync.dma_start(out=tile[:], in_=page1[P * c : P * (c + 1), :])
             return tile
 
         pages = [load_page(0)]
-        w3_raw = [load_rows(w3, b, slice(0, N), "w3_raw_%d" % b, 12288 if b else None) for b in range(2)]
+        w3_raw = [
+            load_rows(wide([P, 4, N], F32, "w3_raw_0"), w3[0:W, 0:N]),
+            load_rows(placed([P, 4, N], F32, AT_W3_RAW, "w3_raw_1"), w3[W : 2 * W, 0:N]),
+        ]
         pages.extend([load_page(c) for c in range(1, 4)])
         idx3 = load_list(offs3, "idx3")
         wg1_tile = held([P, S], F32, "wg1_tile")
         nc.sync.dma_start(out=wg1_tile[:], in_=wg1)
 
+        slices = [(b, t) for b in range(2) for t in range(4)]
         h1 = {}
         sines = {}
 
-        def half_sine(b, t, ch):
+        def half_angle_sine(b, t, half):
             cols = slice(P * t, P * (t + 1))
-            if ch == 0:
+            if half == 0:
                 h1[b, t] = held([P, S], F32, "h1_%d_%d" % (b, t))
-                sines[b, t] = h1[b, t]
-                if (b, t) == (1, 3):
-                    sines[b, t] = reuse.tile([P, S], F32, name="last_sine", align_bytes=64, offset=22528)
-            acc = psum.tile([P, W], F32, tag="x", bufs=4, name="x_%d_%d_%d" % (b, t, ch))
+                last = (b, t) == slices[-1]
+                sines[b, t] = placed([P, S], F32, AT_LAST_SINE, "last_sine") if last else h1[b, t]
+            acc = psum.tile([P, W], F32, tag="x", bufs=BANKS, name="x_%d_%d_%d" % (b, t, half))
             for a in range(2):
                 codes, scales = w1_q[a, b]
                 nc.tensor.matmul_mx(
                     out=acc[:], lhsT=codes[:, cols].bitcast(FP8X4), lhsT_scale=scales[:, cols],
-                    rhs=v_words[a, ch][:].bitcast(FP8X4), rhs_scale=v_plane[ch][4 * a :, :],
+                    rhs=v_words[a, half][:].bitcast(FP8X4), rhs_scale=v_plane[half][4 * a :, :],
                     start=(a == 0), stop=(a == 1),
                 )
-            nc.scalar.activation(sines[b, t][:, W * ch : W * (ch + 1)], acc[:], ACT.Sin, bias=quarter_pi[:], scale=-0.5)
+            nc.scalar.activation(
+                sines[b, t][:, W * half : W * (half + 1)], acc[:], ACT.Sin, bias=quarter_pi[:], scale=-0.5
+            )
 
-        def square(b, t):
-            nc.scalar.activation(h1[b, t][:], sines[b, t][:], ACT.Square)
+        def by_runs(planes, run):
+            return planes.rearrange("p t (c i) -> p c t i", i=run)
 
-        def finish_sine(b, t):
-            if b == 0 and t < ON_SCALAR:
-                nc.scalar.activation(h1[b, t][:], h1[b, t][:], ACT.Copy, bias=1.0, scale=-2.0)
-            else:
-                nc.gpsimd.tensor_scalar(h1[b, t][:], h1[b, t][:], -2.0, 1.0, ALU.mult, ALU.add)
+        def by_runs_grouped(grouped, cols, run):
+            columns = grouped[:].rearrange("p (j t) -> p j t", t=4)[:, cols, :]
+            return columns.rearrange("p (c i) t -> p c t i", i=run)
 
-        def woven(ap3):
-            return ap3.rearrange("p t (c i) -> p c t i", i=4)
-
-        def woven_out(grouped, cols):
-            return grouped[:].rearrange("p (j t) -> p j t", t=4)[:, cols, :].rearrange("p (c i) t -> p c t i", i=4)
-
-        def make_z2(b, picked):
-            grouped = turn([P, 4 * W], BF16, "grouped", 3, "z2_grouped_%d" % b)
+        def make_z2(b):
+            grouped = turn([P, 4 * W], BF16, "grouped", GROUPED_BUFS, "z2_grouped_%d" % b)
             for g in range(4):
                 cols = slice(P * g, P * (g + 1))
-                acc = psum.tile([P, 4, P], F32, tag="x" if b else "late", bufs=4, name="h2_%d_%d" % (b, g))
+                acc = psum.tile([P, 4, P], F32, tag="x" if b else "late", bufs=BANKS, name="h2_%d_%d" % (b, g))
                 for t in range(4):
-                    r0 = W * b + P * t
+                    place = W * b + P * t
                     nc.tensor.matmul_mx(
-                        out=acc[:, t, :], lhsT=w2_dealt[:, 2 * r0 : 2 * (r0 + P)].bitcast(FP4X4),
-                        lhsT_scale=w2_dealt_plane[:, r0 : r0 + P],
+                        out=acc[:, t, :], lhsT=w2_dealt[:, 2 * place : 2 * (place + P)].bitcast(FP4X4),
+                        lhsT_scale=w2_dealt_plane[:, place : place + P],
                         rhs=v2_words[:, cols].bitcast(FP8X4), rhs_scale=v2_plane[:, cols],
                         start=True, stop=True,
                     )
-                nc.vector.tensor_tensor(woven_out(grouped, cols), woven(acc[:]), woven(picked[:, :, cols]), ALU.mult)
+                nc.vector.tensor_tensor(
+                    by_runs_grouped(grouped, cols, 2), by_runs(acc[:], 2), by_runs(picked[b][:, :, cols], 2), ALU.mult
+                )
             return quantize(grouped, "z2_%d" % b)
 
-        z2_q = {}
         for a in range(2):
-            w1_q[a, 1] = quantize(round_w1(w1_raw_late[a], "w1_grouped_%d_1" % a, [nc.vector.tensor_copy]), "w1_%d_1" % a)
-        picked = {0: reuse.tile([P, 4, PK], F32, name="picked_0", align_bytes=64, offset=28672), 1: held([P, 4, PK], F32, "picked_1")}
-        half_sine(0, 0, 0)
-        for b in range(2):
-            for t in range(4):
-                half_sine(b, t, 1)
-                if t < 3 or b == 0:
-                    if t == 3:
-                        half_sine(1, 0, 0)
-                    else:
-                        half_sine(b, t + 1, 0)
-                square(b, t)
-                finish_sine(b, t)
-                nc.vector.tensor_copy(picked[b][:, t, :], h1[b, t][:].indirect(p1[:]))
-            z2_q[b] = make_z2(b, picked[b])
+            grouped = placed([P, 4 * W], BF16, AT_W1_SECOND + 8 * W * a, "w1_grouped_%d_1" % a)
+            round_w1(nc.vector.tensor_copy, grouped, w1_raw[a, 1], 0, P)
+            w1_q[a, 1] = quantize(grouped, "w1_%d_1" % a)
+
+        picked = [placed([P, 4, PK], F32, AT_W1_SECOND, "picked_0"), held([P, 4, PK], F32, "picked_1")]
+        z2_q = {}
+        half_angle_sine(0, 0, 0)
+        for n, (b, t) in enumerate(slices):
+            half_angle_sine(b, t, 1)
+            if n + 1 < len(slices):
+                half_angle_sine(*slices[n + 1], 0)
+            nc.scalar.activation(h1[b, t][:], sines[b, t][:], ACT.Square)
+            if n < AFFINE_ON_SCALAR:
+                nc.scalar.activation(h1[b, t][:], h1[b, t][:], ACT.Copy, bias=1.0, scale=-2.0)
+            else:
+                nc.gpsimd.tensor_scalar(h1[b, t][:], h1[b, t][:], -2.0, 1.0, ALU.mult, ALU.add)
+            nc.vector.tensor_copy(picked[b][:, t, :], h1[b, t][:].indirect(p1[:]))
+            if t == 3:
+                z2_q[b] = make_z2(b)
 
         def second_product(weights, moving, name):
-            acc = psum.tile([P, W], F32, tag="late", bufs=4, name=name)
+            acc = psum.tile([P, W], F32, tag="late", bufs=BANKS, name=name)
             for b in range(2):
                 w_codes, w_scales = weights[b]
                 codes, scales = moving[b]
@@ -264,52 +272,57 @@ def tile_list_excursion_risk_slots_kernel(
                 )
             return acc
 
-        def put(c, offsets, staged, weight):
-            nc.vector.tensor_tensor(pages[c][:].indirect(offsets), staged[:], weight, ALU.mult)
+        def staging(name):
+            return turn([P, W], F32, "staged", STAGED_BUFS, name)
+
+        def put(c, offsets, staged, factor):
+            nc.vector.tensor_tensor(pages[c][:].indirect(offsets), staged[:], factor, ALU.mult)
 
         def stage_y2(c, staged):
             cols = slice(P * c, P * (c + 1))
-            acc = second_product([(w4_codes[:, b, cols], w4_plane[4 * b :, cols]) for b in range(2)], z2_q, "y2_%d" % c)
+            weights = [(w4_codes[:, b, cols], w4_plane[4 * b :, cols]) for b in range(2)]
+            acc = second_product(weights, z2_q, "y2_%d" % c)
             nc.vector.tensor_tensor(staged[:], acc[:], resid_tile[:, c, :], ALU.add)
             return staged
 
-        def stage_y1(ch, c, staged):
+        def put_y1(half, c, staged):
             cols = slice(P * c, P * (c + 1))
-            acc = second_product([(w3_q[b][0][:, cols], w3_q[b][1][:, cols]) for b in range(2)], z1_q[ch], "y1_%d_%d" % (ch, c))
+            weights = [(w3_q[b][0][:, cols], w3_q[b][1][:, cols]) for b in range(2)]
+            acc = second_product(weights, z1_q[half], "y1_%d_%d" % (half, c))
             nc.scalar.copy(out=staged[:], in_=acc[:])
-            return staged
+            put(c, entries(idx3, half), staged, wg1_tile[:, W * half : W * (half + 1)])
 
-        def make_z1(ch):
-            span = slice(W * ch, W * (ch + 1))
+        def make_z1(half):
+            span = slice(W * half, W * (half + 1))
             made = {}
             for b in range(2):
-                rounded = reuse.tile([P, 4, W], BF16, name="z1_rounded_%d_%d" % (ch, b), align_bytes=64, offset=12288 + 4096 * b)
+                rounded = placed([P, 4, W], BF16, AT_W3_RAW + 8 * W * b, "z1_rounded_%d_%d" % (half, b))
                 for t in range(4):
-                    nc.scalar.activation(rounded[:, t, :], h1[b, t][:, span], ACT.Copy, scale=gain_tile[:, b, t : t + 1])
-                if b == 0:
-                    grouped = turn([P, 4 * W], BF16, "grouped", 3, "z1_grouped_%d_%d" % (ch, b))
-                else:
-                    grouped = turn([P, 4 * W], BF16, "last_%d" % ch, 1, "z1_grouped_%d_%d" % (ch, b))
-                nc.scalar.copy(out=woven_out(grouped, slice(0, W)), in_=woven(rounded[:]))
-                made[b] = quantize(grouped, "z1_%d_%d" % (ch, b))
+                    nc.scalar.activation(
+                        rounded[:, t, :], h1[b, t][:, span], ACT.Copy, scale=gain_tile[:, b, t : t + 1]
+                    )
+                tag, bufs = ("grouped", GROUPED_BUFS) if b == 0 else ("last_%d" % half, 1)
+                grouped = turn([P, 4 * W], BF16, tag, bufs, "z1_grouped_%d_%d" % (half, b))
+                nc.scalar.copy(out=by_runs_grouped(grouped, slice(0, W), 4), in_=by_runs(rounded[:], 4))
+                made[b] = quantize(grouped, "z1_%d_%d" % (half, b))
             return made
 
-        y2 = [stage_y2(c, turn([P, W], F32, "staged", 4, "y2_staged_%d" % c)) for c in range(3)]
+        y2 = [stage_y2(c, staging("y2_staged_%d" % c)) for c in range(3)]
         for c in range(3):
             put(c, idx4[:], y2[c], wg2_tile[:])
 
         w3_q = {}
         for b in range(2):
-            grouped = reuse.tile([P, 4 * W], BF16, name="w3_grouped_%d" % b, align_bytes=64, offset=20480 + 4096 * b)
-            nc.scalar.copy(out=woven_out(grouped, slice(0, W)), in_=woven(w3_raw[b][:]))
+            grouped = placed([P, 4 * W], BF16, AT_W3_GROUPED + 8 * W * b, "w3_grouped_%d" % b)
+            nc.scalar.copy(out=by_runs_grouped(grouped, slice(0, W), 4), in_=by_runs(w3_raw[b][:], 4))
             w3_q[b] = quantize(grouped, "w3_%d" % b)
 
         z1_q = {0: make_z1(0)}
         put(3, idx4[:], stage_y2(3, turn([P, W], F32, "last_0", 1, "y2_staged_3")), wg2_tile[:])
         for c in range(3):
-            put(c, idx3[:, 0:32], stage_y1(0, c, turn([P, W], F32, "staged", 4, "y1_staged_0_%d" % c)), wg1_tile[:, 0:W])
+            put_y1(0, c, staging("y1_staged_0_%d" % c))
         z1_q[1] = make_z1(1)
-        put(3, idx3[:, 0:32], stage_y1(0, 3, turn([P, W], F32, "last_1", 1, "y1_staged_0_3")), wg1_tile[:, 0:W])
+        put_y1(0, 3, turn([P, W], F32, "last_1", 1, "y1_staged_0_3"))
         for c in range(4):
-            put(c, idx3[:, 32:64], stage_y1(1, c, turn([P, W], F32, "staged", 4, "y1_staged_1_%d" % c)), wg1_tile[:, W : 2 * W])
+            put_y1(1, c, staging("y1_staged_1_%d" % c))
             nc.sync.dma_start(out=out[P * c : P * (c + 1), :], in_=pages[c][:])

import math
from contextlib import ExitStack

import concourse.mybir as mybir

K, K2, T, S, PK, H, N = 1024, 512, 2048, 1024, 512, 1024, 512
FLOPS = 2 * (K * H * S + K2 * H * PK + H * N * S + H * N * PK)

F32 = mybir.dt.float32
BF16 = mybir.dt.bfloat16
I32 = mybir.dt.int32
U32 = mybir.dt.uint32
U16 = mybir.dt.uint16
U8 = mybir.dt.uint8
FP8X4 = mybir.dt.float8_e4m3fn_x4
FP4X4 = mybir.dt.float4_e2m1fn_x4
ALU = mybir.AluOpType
ACT = mybir.ActivationFunctionType

P = 128
W = 512
LIST_COLUMNS = W // 16
WIDE_BUFS = 7
GROUPED_BUFS = 3
STAGED_BUFS = 4
BANKS = 4
SCALAR_SHARE = 80
AFFINE_ON_SCALAR = 2

AT_W1_FIRST = 0
AT_TAB = 4096
AT_W3_RAW = 12288
AT_W3_GROUPED = 20480
AT_LAST_SINE = AT_W3_GROUPED + 2048
AT_W1_SECOND = 28672


def tile_list_excursion_risk_slots_kernel(
    tc, tab_words, tab_scales, tab2_words, tab2_scales, offs, offs2, pos1, offs3, offs4,
    w1, w2_words, w2_scales, gain, w3, w4_words, w4_scales, resid, page1, wg1, wg2, out,
):
    nc = tc.nc
    with ExitStack() as ctx:
        keep = ctx.enter_context(tc.tile_pool(name="keep", bufs=1))
        ring = ctx.enter_context(tc.tile_pool(name="ring", bufs=2))
        reuse = ctx.enter_context(tc.tile_pool(name="reuse", bufs=1))
        psum = ctx.enter_context(tc.psum_pool(name="psum", bufs=1))

        def held(shape, dtype, name):
            return keep.tile(shape, dtype, name=name, align_bytes=64)

        def turn(shape, dtype, tag, bufs, name):
            return ring.tile(shape, dtype, tag=tag, bufs=bufs, name=name, align_bytes=64)

        def placed(shape, dtype, offset, name):
            return reuse.tile(shape, dtype, name=name, align_bytes=64, offset=offset)

        def wide(shape, dtype, name):
            return turn(shape, dtype, "wide", WIDE_BUFS, name)

        def entries(offsets, half):
            return offsets[:, LIST_COLUMNS * half : LIST_COLUMNS * (half + 1)]

        def load_list(src, name):
            tile = keep.tile(list(src.shape), U16, name=name)
            nc.sync.dma_start(tile[:], src)
            return tile

        def zeroed_plane(src, name, engine):
            plane = held([P, src.shape[2]], U8, name)
            engine.memset(plane[:].bitcast(I32), 0)
            return plane

        def load_plane(plane, src):
            for q in range(4):
                nc.sync.dma_start(
                    out=plane[32 * q : 32 * q + 4 * src.shape[0], :].bitcast(I32),
                    in_=src[:, 4 * q : 4 * q + 4, :].bitcast(I32),
                )

        def load_words(tile, src):
            nc.sync.dma_start(out=tile[:], in_=src.rearrange("p t i -> p (t i)").bitcast(I32))
            return tile

        def load_rows(tile, src):
            nc.sync.dma_start(out=tile[:], in_=src.rearrange("(p j) c -> p j c", j=4))
            return tile

        def quantize(grouped, name):
            codes = held([P, W], U32, name + "_codes")
            scales = held([P, W], U8, name + "_scales")
            nc.vector.quantize_mx(out=codes[:].bitcast(FP8X4), scales=scales[:], in_=grouped[:])
            return codes, scales

        def gather(into, window, offsets):
            nc.vector.tensor_copy(into[:], window.indirect(offsets))
            return into

        tab_plane = zeroed_plane(tab_scales, "tab_plane", nc.vector)
        w2_plane = zeroed_plane(w2_scales, "w2_plane", nc.gpsimd)
        tab2_plane = zeroed_plane(tab2_scales, "tab2_plane", nc.gpsimd)
        w4_plane = zeroed_plane(w4_scales, "w4_plane", nc.gpsimd)

        zero = keep.tile([P, 1], F32, name="zero")
        sine_of_zero = keep.tile([P, 1], F32, name="sine_of_zero")
        quarter_pi = keep.tile([P, 1], F32, name="quarter_pi")
        nc.gpsimd.memset(zero[:], 0.0)
        nc.scalar.activation(sine_of_zero[:], zero[:], ACT.Sin)
        nc.gpsimd.tensor_scalar(quarter_pi[:], sine_of_zero[:], 1.0, math.pi / 4, ALU.mult, ALU.add)

        idx = load_list(offs, "idx")
        w2_raw = held([P, 2 * H], U8, "w2_raw")
        nc.sync.dma_start(out=w2_raw[:].bitcast(I32), in_=w2_words[0].bitcast(I32))
        w2_dealt = held([P, 2 * H], U8, "w2_dealt")
        for b in range(2):
            nc.vector.tensor_copy(
                out=w2_dealt[:, 2 * W * b : 2 * W * (b + 1)].rearrange("p (t m e) -> p t m e", t=4, e=2),
                in_=w2_raw[:, 2 * W * b : 2 * W * (b + 1)].rearrange("p (m t e) -> p t m e", t=4, e=2),
            )

        def load_w1(a, b):
            tile = wide([P, 4, W], F32, "w1_raw_%d_%d" % (a, b))
            return load_rows(tile, w1[W * a : W * (a + 1), W * b : W * (b + 1)])

        tab_tiles = [load_words(wide([P, T], I32, "tab_0"), tab_words[0])]
        load_plane(tab_plane, tab_scales)
        w1_raw = {(a, 0): load_w1(a, 0) for a in range(2)}
        tab_tiles.append(load_words(placed([P, T], I32, AT_TAB, "tab_1"), tab_words[1]))
        load_plane(w2_plane, w2_scales)
        idx2 = load_list(offs2, "idx2")
        tab2_tile = load_words(wide([P, T], I32, "tab2"), tab2_words[0])
        load_plane(tab2_plane, tab2_scales)
        p1 = load_list(pos1, "p1")
        for a in range(2):
            w1_raw[a, 1] = load_w1(a, 1)

        def round_w1(copy, grouped, raw, m0, m1):
            copy(
                out=grouped[:].rearrange("p (t m j) -> p m j t", t=4, j=4)[:, m0:m1],
                in_=raw[:].rearrange("p j (m t) -> p m j t", t=4)[:, m0:m1],
            )

        v_words = {}
        v_plane = {}
        w1_q = {}
        for half in range(2):
            into = held([P, W], U32, "v_words_0_%d" % half)
            v_words[0, half] = gather(into, tab_tiles[0][:].bitcast(U32), entries(idx, half))
        for half in range(2):
            v_plane[half] = gather(held([P, W], U8, "v_plane_%d" % half), tab_plane[:], entries(idx, half))
        grouped = turn([P, 4 * W], BF16, "grouped", GROUPED_BUFS, "w1_grouped_0_0")
        round_w1(nc.scalar.copy, grouped, w1_raw[0, 0], 0, P)
        w1_q[0, 0] = quantize(grouped, "w1_0_0")
        grouped = placed([P, 4 * W], BF16, AT_W1_FIRST, "w1_grouped_1_0")
        round_w1(nc.scalar.copy, grouped, w1_raw[1, 0], 0, SCALAR_SHARE)
        round_w1(nc.vector.tensor_copy, grouped, w1_raw[1, 0], SCALAR_SHARE, P)
        w1_q[1, 0] = quantize(grouped, "w1_1_0")
        for half in range(2):
            into = placed([P, W], U32, AT_W1_FIRST + 4 * W * half, "v_words_1_%d" % half)
            v_words[1, half] = gather(into, tab_tiles[1][:].bitcast(U32), entries(idx, half))

        w2_dealt_plane = placed([P, H], U8, AT_TAB + 5 * W, "w2_dealt_plane")
        nc.vector.tensor_copy(
            out=w2_dealt_plane[:].rearrange("p (b t m) -> p b t m", b=2, t=4),
            in_=w2_plane[:].rearrange("p (b m t) -> p b t m", b=2, t=4),
        )
        v2_words = gather(placed([P, PK], U32, AT_TAB, "v2_words"), tab2_tile[:].bitcast(U32), idx2[:])
        v2_plane = gather(placed([P, PK], U8, AT_TAB + 4 * W, "v2_plane"), tab2_plane[:], idx2[:])

        idx4 = load_list(offs4, "idx4")
        w4_codes = held([P, 2, N], I32, "w4_codes")
        nc.sync.dma_start(out=w4_codes[:], in_=w4_words.rearrange("a p c i -> p a (c i)").bitcast(I32))
        load_plane(w4_plane, w4_scales)
        resid_tile = wide([P, 4, PK], F32, "resid_tile")
        nc.sync.dma_start(out=resid_tile[:], in_=resid.rearrange("(c p) j -> p c j", p=P))
        wg2_tile = held([P, PK], F32, "wg2_tile")
        nc.sync.dma_start(out=wg2_tile[:], in_=wg2)
        gain_tile = held([P, 2, 4], F32, "gain_tile")
        nc.sync.dma_start(out=gain_tile[:], in_=gain.rearrange("(b p t) -> p b t", b=2, t=4))

        def load_page(c):
            tile = wide([P, T], F32, "page_%d" % c)
            nc.sync.dma_start(out=tile[:], in_=page1[P * c : P * (c + 1), :])
            return tile

        pages = [load_page(0)]
        w3_raw = [
            load_rows(wide([P, 4, N], F32, "w3_raw_0"), w3[0:W, 0:N]),
            load_rows(placed([P, 4, N], F32, AT_W3_RAW, "w3_raw_1"), w3[W : 2 * W, 0:N]),
        ]
        pages.extend([load_page(c) for c in range(1, 4)])
        idx3 = load_list(offs3, "idx3")
        wg1_tile = held([P, S], F32, "wg1_tile")
        nc.sync.dma_start(out=wg1_tile[:], in_=wg1)

        slices = [(b, t) for b in range(2) for t in range(4)]
        h1 = {}
        sines = {}

        def half_angle_sine(b, t, half):
            cols = slice(P * t, P * (t + 1))
            if half == 0:
                h1[b, t] = held([P, S], F32, "h1_%d_%d" % (b, t))
                last = (b, t) == slices[-1]
                sines[b, t] = placed([P, S], F32, AT_LAST_SINE, "last_sine") if last else h1[b, t]
            acc = psum.tile([P, W], F32, tag="x", bufs=BANKS, name="x_%d_%d_%d" % (b, t, half))
            for a in range(2):
                codes, scales = w1_q[a, b]
                nc.tensor.matmul_mx(
                    out=acc[:], lhsT=codes[:, cols].bitcast(FP8X4), lhsT_scale=scales[:, cols],
                    rhs=v_words[a, half][:].bitcast(FP8X4), rhs_scale=v_plane[half][4 * a :, :],
                    start=(a == 0), stop=(a == 1),
                )
            nc.scalar.activation(
                sines[b, t][:, W * half : W * (half + 1)], acc[:], ACT.Sin, bias=quarter_pi[:], scale=-0.5
            )

        def by_runs(planes, run):
            return planes.rearrange("p t (c i) -> p c t i", i=run)

        def by_runs_grouped(grouped, cols, run):
            columns = grouped[:].rearrange("p (j t) -> p j t", t=4)[:, cols, :]
            return columns.rearrange("p (c i) t -> p c t i", i=run)

        def make_z2(b):
            grouped = turn([P, 4 * W], BF16, "grouped", GROUPED_BUFS, "z2_grouped_%d" % b)
            for g in range(4):
                cols = slice(P * g, P * (g + 1))
                acc = psum.tile([P, 4, P], F32, tag="x" if b else "late", bufs=BANKS, name="h2_%d_%d" % (b, g))
                for t in range(4):
                    place = W * b + P * t
                    nc.tensor.matmul_mx(
                        out=acc[:, t, :], lhsT=w2_dealt[:, 2 * place : 2 * (place + P)].bitcast(FP4X4),
                        lhsT_scale=w2_dealt_plane[:, place : place + P],
                        rhs=v2_words[:, cols].bitcast(FP8X4), rhs_scale=v2_plane[:, cols],
                        start=True, stop=True,
                    )
                nc.vector.tensor_tensor(
                    by_runs_grouped(grouped, cols, 2), by_runs(acc[:], 2), by_runs(picked[b][:, :, cols], 2), ALU.mult
                )
            return quantize(grouped, "z2_%d" % b)

        for a in range(2):
            grouped = placed([P, 4 * W], BF16, AT_W1_SECOND + 8 * W * a, "w1_grouped_%d_1" % a)
            round_w1(nc.vector.tensor_copy, grouped, w1_raw[a, 1], 0, P)
            w1_q[a, 1] = quantize(grouped, "w1_%d_1" % a)

        picked = [placed([P, 4, PK], F32, AT_W1_SECOND, "picked_0"), held([P, 4, PK], F32, "picked_1")]
        z2_q = {}
        half_angle_sine(0, 0, 0)
        for n, (b, t) in enumerate(slices):
            half_angle_sine(b, t, 1)
            if n + 1 < len(slices):
                half_angle_sine(*slices[n + 1], 0)
            nc.scalar.activation(h1[b, t][:], sines[b, t][:], ACT.Square)
            if n < AFFINE_ON_SCALAR:
                nc.scalar.activation(h1[b, t][:], h1[b, t][:], ACT.Copy, bias=1.0, scale=-2.0)
            else:
                nc.gpsimd.tensor_scalar(h1[b, t][:], h1[b, t][:], -2.0, 1.0, ALU.mult, ALU.add)
            nc.vector.tensor_copy(picked[b][:, t, :], h1[b, t][:].indirect(p1[:]))
            if t == 3:
                z2_q[b] = make_z2(b)

        def second_product(weights, moving, name):
            acc = psum.tile([P, W], F32, tag="late", bufs=BANKS, name=name)
            for b in range(2):
                w_codes, w_scales = weights[b]
                codes, scales = moving[b]
                nc.tensor.matmul_mx(
                    out=acc[:], lhsT=w_codes.bitcast(FP8X4), lhsT_scale=w_scales,
                    rhs=codes[:].bitcast(FP8X4), rhs_scale=scales[:], start=(b == 0), stop=(b == 1),
                )
            return acc

        def staging(name):
            return turn([P, W], F32, "staged", STAGED_BUFS, name)

        def put(c, offsets, staged, factor):
            nc.vector.tensor_tensor(pages[c][:].indirect(offsets), staged[:], factor, ALU.mult)

        def stage_y2(c, staged):
            cols = slice(P * c, P * (c + 1))
            weights = [(w4_codes[:, b, cols], w4_plane[4 * b :, cols]) for b in range(2)]
            acc = second_product(weights, z2_q, "y2_%d" % c)
            nc.vector.tensor_tensor(staged[:], acc[:], resid_tile[:, c, :], ALU.add)
            return staged

        def put_y1(half, c, staged):
            cols = slice(P * c, P * (c + 1))
            weights = [(w3_q[b][0][:, cols], w3_q[b][1][:, cols]) for b in range(2)]
            acc = second_product(weights, z1_q[half], "y1_%d_%d" % (half, c))
            nc.scalar.copy(out=staged[:], in_=acc[:])
            put(c, entries(idx3, half), staged, wg1_tile[:, W * half : W * (half + 1)])

        def make_z1(half):
            span = slice(W * half, W * (half + 1))
            made = {}
            for b in range(2):
                rounded = placed([P, 4, W], BF16, AT_W3_RAW + 8 * W * b, "z1_rounded_%d_%d" % (half, b))
                for t in range(4):
                    nc.scalar.activation(
                        rounded[:, t, :], h1[b, t][:, span], ACT.Copy, scale=gain_tile[:, b, t : t + 1]
                    )
                tag, bufs = ("grouped", GROUPED_BUFS) if b == 0 else ("last_%d" % half, 1)
                grouped = turn([P, 4 * W], BF16, tag, bufs, "z1_grouped_%d_%d" % (half, b))
                nc.scalar.copy(out=by_runs_grouped(grouped, slice(0, W), 4), in_=by_runs(rounded[:], 4))
                made[b] = quantize(grouped, "z1_%d_%d" % (half, b))
            return made

        y2 = [stage_y2(c, staging("y2_staged_%d" % c)) for c in range(3)]
        for c in range(3):
            put(c, idx4[:], y2[c], wg2_tile[:])

        w3_q = {}
        for b in range(2):
            grouped = placed([P, 4 * W], BF16, AT_W3_GROUPED + 8 * W * b, "w3_grouped_%d" % b)
            nc.scalar.copy(out=by_runs_grouped(grouped, slice(0, W), 4), in_=by_runs(w3_raw[b][:], 4))
            w3_q[b] = quantize(grouped, "w3_%d" % b)

        z1_q = {0: make_z1(0)}
        put(3, idx4[:], stage_y2(3, turn([P, W], F32, "last_0", 1, "y2_staged_3")), wg2_tile[:])
        for c in range(3):
            put_y1(0, c, staging("y1_staged_0_%d" % c))
        z1_q[1] = make_z1(1)
        put_y1(0, 3, turn([P, W], F32, "last_1", 1, "y1_staged_0_3"))
        for c in range(4):
            put_y1(1, c, staging("y1_staged_1_%d" % c))
            nc.sync.dma_start(out=out[P * c : P * (c + 1), :], in_=pages[c][:])
